import numpy as np
import ml_dtypes

BF16 = ml_dtypes.bfloat16


def bf(x):
    return np.asarray(x, np.float32).astype(BF16)


def f32(x):
    return np.asarray(x, np.float32)


def f64(x):
    return np.asarray(x).astype(np.float64)


def striped(idx):
    return np.concatenate([l.reshape(-1, 16).T for l in idx])


def rows(idx, k):
    return np.tile(np.repeat(idx, 16, axis=0), (k // (16 * 8), 1))


def look(tab, idx):
    return np.take_along_axis(f64(tab), rows(idx, len(tab)), axis=1)


K, S, H, D, V, N = 128, 2048, 256, 3, 512, 1536


def setup_inputs():
    return {"z": bf(np.random.standard_normal((H, S))), "wt": bf(np.random.standard_normal((H, K)) / np.sqrt(H)), "u0": f32(np.random.uniform(0.2, 1.0, (K, V))), "u1": f32(np.random.uniform(0.2, 1.0, (K, V))), "u2": f32(np.random.uniform(0.2, 1.0, (K, V))), "offs": striped(np.stack([np.random.permutation(S)[:N] for _ in range(8)]))}


def reference(z, wt, u0, u1, u2, offs):
    idx = np.stack([g.T.reshape(-1) for g in np.split(offs, 8)])
    tab = f64(wt).T @ f64(z)
    x = f64(u0) * look(tab, idx[:, :V]) + f64(u1) * look(tab, idx[:, 1 * V:2 * V]) + f64(u2) * look(tab, idx[:, 2 * V:3 * V])
    return x

@@ -1,0 +1,55 @@
+import concourse.mybir as mybir
+
+BF16, F32, U16 = mybir.dt.bfloat16, mybir.dt.float32, mybir.dt.uint16
+MULT, ADD = mybir.AluOpType.mult, mybir.AluOpType.add
+
+P = 128
+BANK = 512
+LANES = 16
+
+FLOPS = 2 * 256 * 128 * 2048 + 5 * 128 * 512
+
+
+def tile_lookup_pjmix_out_kernel(tc, z, wt, u0, u1, u2, offs, out):
+    nc = tc.nc
+    features, places = z.shape
+    width = out.shape[1]
+    k_blocks = features // P
+    z_blocks = z.rearrange("(h p) s -> p h s", p=P)
+
+    with (
+        tc.tile_pool(name="held", bufs=1) as held,
+        tc.psum_pool(name="psum", bufs=1) as psum,
+    ):
+        offsets = held.tile([P, offs.shape[1]], U16, name="offsets")
+        nc.sync.dma_start(offsets[:], offs)
+        weights = held.tile([P, k_blocks, P], BF16, name="weights")
+        nc.sync.dma_start(weights[:], wt.rearrange("(h p) r -> p h r", p=P))
+
+        table = held.tile([P, places], F32, name="table")
+        for c in range(places // BANK):
+            cols = slice(c * BANK, (c + 1) * BANK)
+            z_part = held.tile([P, k_blocks, BANK], BF16, name=f"z_part{c}")
+            nc.sync.dma_start(z_part[:], z_blocks[:, :, cols])
+            bank = psum.tile([P, BANK], F32, name=f"bank{c}")
+            for h in range(k_blocks):
+                nc.tensor.matmul(bank[:], weights[:, h, :], z_part[:, h, :], start=h == 0, stop=h == k_blocks - 1)
+            if c % 2 == 0:
+                nc.scalar.copy(table[:, cols], bank[:])
+            else:
+                nc.vector.tensor_copy(table[:, cols], bank[:])
+
+        products = []
+        for d, u in enumerate((u0, u1, u2)):
+            mix = held.tile([P, width], F32, name=f"mix{d}")
+            nc.sync.dma_start(mix[:], u)
+            product = held.tile([P, width], F32, name=f"product{d}")
+            piece = offsets[:, d * width // LANES : (d + 1) * width // LANES]
+            nc.vector.tensor_tensor(product[:], table[:].indirect(piece), mix[:], MULT)
+            products.append(product)
+
+        partial = held.tile([P, width], F32, name="partial")
+        nc.vector.tensor_tensor(partial[:], products[0][:], products[1][:], ADD)
+        total = held.tile([P, width], F32, name="total")
+        nc.vector.tensor_tensor(total[:], partial[:], products[2][:], ADD)
+        nc.sync.dma_start(out, total[:])

@@ -4,8 +4,12 @@ BF16, F32, U16 = mybir.dt.bfloat16, mybir.dt.float32, mybir.dt.uint16
 MULT, ADD = mybir.AluOpType.mult, mybir.AluOpType.add
 
 P = 128
-BANK = 512
 LANES = 16
+PSUM_BANKS = 8
+SPAN = 256
+LOADS = (1024, 512, 512)
+STORES = 2
+WARM_MATMULS = 16
 
 FLOPS = 2 * 256 * 128 * 2048 + 5 * 128 * 512
 
@@ -15,41 +19,58 @@ def tile_lookup_pjmix_out_kernel(tc, z, wt, u0, u1, u2, offs, out):
     features, places = z.shape
     width = out.shape[1]
     k_blocks = features // P
-    z_blocks = z.rearrange("(h p) s -> p h s", p=P)
+    z_blocks = z.rearrange("(p h) s -> p h s", p=P)
 
     with (
         tc.tile_pool(name="held", bufs=1) as held,
-        tc.psum_pool(name="psum", bufs=1) as psum,
+        tc.psum_pool(name="psum", bufs=PSUM_BANKS) as psum,
     ):
-        offsets = held.tile([P, offs.shape[1]], U16, name="offsets")
-        nc.sync.dma_start(offsets[:], offs)
         weights = held.tile([P, k_blocks, P], BF16, name="weights")
-        nc.sync.dma_start(weights[:], wt.rearrange("(h p) r -> p h r", p=P))
+        nc.scalar.dma_start(weights[:], wt.rearrange("(p h) r -> p h r", p=P))
+
+        zeros = held.tile([P, P], BF16, name="zeros")
+        nc.vector.memset(zeros[:], 0.0)
+        warm = psum.tile([P, P], F32, name="warm", tag="bank")
+        for i in range(WARM_MATMULS):
+            nc.tensor.matmul(warm[:], zeros[:], zeros[:], start=True, stop=True)
 
         table = held.tile([P, places], F32, name="table")
-        for c in range(places // BANK):
-            cols = slice(c * BANK, (c + 1) * BANK)
-            z_part = held.tile([P, k_blocks, BANK], BF16, name=f"z_part{c}")
-            nc.sync.dma_start(z_part[:], z_blocks[:, :, cols])
-            bank = psum.tile([P, BANK], F32, name=f"bank{c}")
+        first = 0
+        for load in LOADS:
+            spans = range(first, first + load, SPAN)
+            banks = [psum.tile([P, SPAN], F32, name=f"bank{s}", tag="bank") for s in spans]
             for h in range(k_blocks):
-                nc.tensor.matmul(bank[:], weights[:, h, :], z_part[:, h, :], start=h == 0, stop=h == k_blocks - 1)
-            if c % 2 == 0:
-                nc.scalar.copy(table[:, cols], bank[:])
-            else:
-                nc.vector.tensor_copy(table[:, cols], bank[:])
+                z_part = held.tile([P, load], BF16, name=f"z_part{first}_{h}")
+                nc.sync.dma_start(z_part[:], z_blocks[:, h, first : first + load])
+                for i, bank in enumerate(banks):
+                    nc.tensor.matmul(bank[:], weights[:, h, :], z_part[:, i * SPAN : (i + 1) * SPAN],
+                                     start=h == 0, stop=h == k_blocks - 1)
+            for i, s in enumerate(spans):
+                if i % 2 == 0:
+                    nc.scalar.copy(table[:, s : s + SPAN], banks[i][:])
+                else:
+                    nc.vector.tensor_copy(table[:, s : s + SPAN], banks[i][:])
+            first += load
 
-        products = []
+        offsets = held.tile([P, offs.shape[1]], U16, name="offsets")
+        nc.sync.dma_start(offsets[:], offs)
+
+        mixes = []
         for d, u in enumerate((u0, u1, u2)):
             mix = held.tile([P, width], F32, name=f"mix{d}")
             nc.sync.dma_start(mix[:], u)
-            product = held.tile([P, width], F32, name=f"product{d}")
-            piece = offsets[:, d * width // LANES : (d + 1) * width // LANES]
-            nc.vector.tensor_tensor(product[:], table[:].indirect(piece), mix[:], MULT)
-            products.append(product)
+            mixes.append(mix)
+
+        def look_up(d, lo, hi):
+            product = held.tile([P, hi - lo], F32, name=f"product{d}_{lo}")
+            piece = offsets[:, (d * width + lo) // LANES : (d * width + hi) // LANES]
+            nc.vector.tensor_tensor(product[:], table[:].indirect(piece), mixes[d][:, lo:hi], MULT)
+            return product
 
         partial = held.tile([P, width], F32, name="partial")
-        nc.vector.tensor_tensor(partial[:], products[0][:], products[1][:], ADD)
-        total = held.tile([P, width], F32, name="total")
-        nc.vector.tensor_tensor(total[:], partial[:], products[2][:], ADD)
-        nc.sync.dma_start(out, total[:])
+        nc.vector.tensor_tensor(partial[:], look_up(0, 0, width)[:], look_up(1, 0, width)[:], ADD)
+        for lo in range(0, width, width // STORES):
+            hi = lo + width // STORES
+            total = held.tile([P, hi - lo], F32, name=f"total{lo}")
+            nc.vector.tensor_tensor(total[:], partial[:, lo:hi], look_up(2, lo, hi)[:], ADD)
+            nc.sync.dma_start(out[:, lo:hi], total[:])

@@ -1,15 +1,15 @@
 import concourse.mybir as mybir
+from concourse.masks import make_identity
 
 BF16, F32, U16 = mybir.dt.bfloat16, mybir.dt.float32, mybir.dt.uint16
 MULT, ADD = mybir.AluOpType.mult, mybir.AluOpType.add
 
 P = 128
 LANES = 16
-PSUM_BANKS = 8
-SPAN = 256
 LOADS = (1024, 512, 512)
-STORES = 2
+HALVES = 2
 WARM_MATMULS = 16
+KEEP_WARM_MATMULS = 8
 
 FLOPS = 2 * 256 * 128 * 2048 + 5 * 128 * 512
 
@@ -18,39 +18,40 @@ def tile_lookup_pjmix_out_kernel(tc, z, wt, u0, u1, u2, offs, out):
     nc = tc.nc
     features, places = z.shape
     width = out.shape[1]
+    half = width // HALVES
     k_blocks = features // P
     z_blocks = z.rearrange("(p h) s -> p h s", p=P)
 
     with (
         tc.tile_pool(name="held", bufs=1) as held,
-        tc.psum_pool(name="psum", bufs=PSUM_BANKS) as psum,
+        tc.psum_pool(name="psum", bufs=1) as psum,
     ):
         weights = held.tile([P, k_blocks, P], BF16, name="weights")
         nc.scalar.dma_start(weights[:], wt.rearrange("(p h) r -> p h r", p=P))
+        partials = [psum.tile([P, half], F32, name=f"partial{i}") for i in range(HALVES)]
 
         zeros = held.tile([P, P], BF16, name="zeros")
         nc.vector.memset(zeros[:], 0.0)
-        warm = psum.tile([P, P], F32, name="warm", tag="bank")
         for i in range(WARM_MATMULS):
-            nc.tensor.matmul(warm[:], zeros[:], zeros[:], start=True, stop=True)
+            nc.tensor.matmul(partials[0][:, :P], zeros[:], zeros[:], start=True, stop=True)
 
         table = held.tile([P, places], F32, name="table")
         first = 0
         for load in LOADS:
-            spans = range(first, first + load, SPAN)
-            banks = [psum.tile([P, SPAN], F32, name=f"bank{s}", tag="bank") for s in spans]
+            span = load // 2
+            banks = [psum.tile([P, span], F32, name=f"bank{first}_{i}") for i in range(2)]
             for h in range(k_blocks):
                 z_part = held.tile([P, load], BF16, name=f"z_part{first}_{h}")
                 nc.sync.dma_start(z_part[:], z_blocks[:, h, first : first + load])
                 for i, bank in enumerate(banks):
-                    nc.tensor.matmul(bank[:], weights[:, h, :], z_part[:, i * SPAN : (i + 1) * SPAN],
+                    nc.tensor.matmul(bank[:], weights[:, h, :], z_part[:, i * span : (i + 1) * span],
                                      start=h == 0, stop=h == k_blocks - 1)
-            for i, s in enumerate(spans):
-                if i % 2 == 0:
-                    nc.scalar.copy(table[:, s : s + SPAN], banks[i][:])
-                else:
-                    nc.vector.tensor_copy(table[:, s : s + SPAN], banks[i][:])
+            nc.scalar.copy(table[:, first : first + span], banks[0][:])
+            nc.vector.tensor_copy(table[:, first + span : first + load], banks[1][:])
             first += load
+
+        for i in range(KEEP_WARM_MATMULS):
+            nc.tensor.matmul(partials[0][:], zeros[:], z_part[:, :half], start=True, stop=True)
 
         offsets = held.tile([P, offs.shape[1]], U16, name="offsets")
         nc.sync.dma_start(offsets[:], offs)
@@ -61,16 +62,21 @@ def tile_lookup_pjmix_out_kernel(tc, z, wt, u0, u1, u2, offs, out):
             nc.sync.dma_start(mix[:], u)
             mixes.append(mix)
 
-        def look_up(d, lo, hi):
-            product = held.tile([P, hi - lo], F32, name=f"product{d}_{lo}")
-            piece = offsets[:, (d * width + lo) // LANES : (d * width + hi) // LANES]
-            nc.vector.tensor_tensor(product[:], table[:].indirect(piece), mixes[d][:, lo:hi], MULT)
+        def look_up(d, i):
+            product = held.tile([P, half], F32, name=f"product{d}_{i}")
+            entry = d * width + i * half
+            piece = offsets[:, entry // LANES : (entry + half) // LANES]
+            nc.vector.tensor_tensor(product[:], table[:].indirect(piece), mixes[d][:, i * half : (i + 1) * half], MULT)
             return product
 
-        partial = held.tile([P, width], F32, name="partial")
-        nc.vector.tensor_tensor(partial[:], look_up(0, 0, width)[:], look_up(1, 0, width)[:], ADD)
-        for lo in range(0, width, width // STORES):
-            hi = lo + width // STORES
-            total = held.tile([P, hi - lo], F32, name=f"total{lo}")
-            nc.vector.tensor_tensor(total[:], partial[:, lo:hi], look_up(2, lo, hi)[:], ADD)
-            nc.sync.dma_start(out[:, lo:hi], total[:])
+        identity = held.tile([P, P], F32, name="identity")
+        make_identity(nc, identity[:])
+
+        for d in range(2):
+            for i in range(HALVES):
+                nc.tensor.matmul(partials[i][:], identity[:], look_up(d, i)[:], start=d == 0, stop=d == 1)
+        lasts = [look_up(2, i) for i in range(HALVES)]
+        for i in range(HALVES):
+            total = held.tile([P, half], F32, name=f"total{i}")
+            nc.vector.tensor_tensor(total[:], partials[i][:], lasts[i][:], ADD)
+            nc.sync.dma_start(out[:, i * half : (i + 1) * half], total[:])

@@ -5,8 +5,9 @@ BF16, F32, U16 = mybir.dt.bfloat16, mybir.dt.float32, mybir.dt.uint16
 MULT, ADD = mybir.AluOpType.mult, mybir.AluOpType.add
 
 P = 128
-LANES = 16
-LOADS = (1024, 512, 512)
+ENTRIES_PER_COLUMN = 16
+PSUM_BANKS = 8
+RUNS = (1024, 512, 256, 256)
 HALVES = 2
 WARM_MATMULS = 16
 KEEP_WARM_MATMULS = 8
@@ -24,57 +25,54 @@ def tile_lookup_pjmix_out_kernel(tc, z, wt, u0, u1, u2, offs, out):
 
     with (
         tc.tile_pool(name="held", bufs=1) as held,
-        tc.psum_pool(name="psum", bufs=1) as psum,
+        tc.psum_pool(name="psum", bufs=PSUM_BANKS) as psum,
     ):
-        weights = held.tile([P, k_blocks, P], BF16, name="weights")
-        nc.scalar.dma_start(weights[:], wt.rearrange("(p h) r -> p h r", p=P))
-        partials = [psum.tile([P, half], F32, name=f"partial{i}") for i in range(HALVES)]
+        projection = held.tile([P, k_blocks, P], BF16, name="projection")
+        nc.scalar.dma_start(projection[:], wt.rearrange("(p h) r -> p h r", p=P))
 
         zeros = held.tile([P, P], BF16, name="zeros")
         nc.vector.memset(zeros[:], 0.0)
+        warm = psum.tile([P, half], F32, name="warm", tag="bank")
         for i in range(WARM_MATMULS):
-            nc.tensor.matmul(partials[0][:, :P], zeros[:], zeros[:], start=True, stop=True)
+            nc.tensor.matmul(warm[:, :P], zeros[:], zeros[:], start=True, stop=True)
 
         table = held.tile([P, places], F32, name="table")
         first = 0
-        for load in LOADS:
-            span = load // 2
-            banks = [psum.tile([P, span], F32, name=f"bank{first}_{i}") for i in range(2)]
+        for run in RUNS:
+            span = run // 2
+            banks = [psum.tile([P, span], F32, name=f"bank{first}_{i}", tag="bank") for i in range(2)]
             for h in range(k_blocks):
-                z_part = held.tile([P, load], BF16, name=f"z_part{first}_{h}")
-                nc.sync.dma_start(z_part[:], z_blocks[:, h, first : first + load])
+                z_part = held.tile([P, run], BF16, name=f"z_part{first}_{h}")
+                nc.sync.dma_start(z_part[:], z_blocks[:, h, first : first + run])
                 for i, bank in enumerate(banks):
-                    nc.tensor.matmul(bank[:], weights[:, h, :], z_part[:, i * span : (i + 1) * span],
+                    nc.tensor.matmul(bank[:], projection[:, h, :], z_part[:, i * span : (i + 1) * span],
                                      start=h == 0, stop=h == k_blocks - 1)
-            nc.scalar.copy(table[:, first : first + span], banks[0][:])
-            nc.vector.tensor_copy(table[:, first + span : first + load], banks[1][:])
-            first += load
+            nc.vector.tensor_copy(table[:, first : first + span], banks[0][:])
+            nc.scalar.copy(table[:, first + span : first + run], banks[1][:])
+            first += run
 
         for i in range(KEEP_WARM_MATMULS):
-            nc.tensor.matmul(partials[0][:], zeros[:], z_part[:, :half], start=True, stop=True)
+            nc.tensor.matmul(warm[:], zeros[:], z_part[:, :half], start=True, stop=True)
 
         offsets = held.tile([P, offs.shape[1]], U16, name="offsets")
-        nc.sync.dma_start(offsets[:], offs)
-
-        mixes = []
-        for d, u in enumerate((u0, u1, u2)):
-            mix = held.tile([P, width], F32, name=f"mix{d}")
-            nc.sync.dma_start(mix[:], u)
-            mixes.append(mix)
+        mixes = [held.tile([P, width], F32, name=f"mix{d}") for d in range(3)]
+        for tile, source in ((mixes[0], u0), (offsets, offs), (mixes[1], u1), (mixes[2], u2)):
+            nc.sync.dma_start(tile[:], source)
 
         def look_up(d, i):
             product = held.tile([P, half], F32, name=f"product{d}_{i}")
             entry = d * width + i * half
-            piece = offsets[:, entry // LANES : (entry + half) // LANES]
+            piece = offsets[:, entry // ENTRIES_PER_COLUMN : (entry + half) // ENTRIES_PER_COLUMN]
             nc.vector.tensor_tensor(product[:], table[:].indirect(piece), mixes[d][:, i * half : (i + 1) * half], MULT)
             return product
 
         identity = held.tile([P, P], F32, name="identity")
         make_identity(nc, identity[:])
-
+        partials = [psum.tile([P, half], F32, name=f"partial{i}", tag="bank") for i in range(HALVES)]
         for d in range(2):
             for i in range(HALVES):
                 nc.tensor.matmul(partials[i][:], identity[:], look_up(d, i)[:], start=d == 0, stop=d == 1)
+
         lasts = [look_up(2, i) for i in range(HALVES)]
         for i in range(HALVES):
             total = held.tile([P, half], F32, name=f"total{i}")

import concourse.mybir as mybir
from concourse.masks import make_identity

BF16, F32, U16 = mybir.dt.bfloat16, mybir.dt.float32, mybir.dt.uint16
MULT, ADD = mybir.AluOpType.mult, mybir.AluOpType.add

P = 128
ENTRIES_PER_COLUMN = 16
PSUM_BANKS = 8
RUNS = (1024, 512, 256, 256)
HALVES = 2
WARM_MATMULS = 16
KEEP_WARM_MATMULS = 8

FLOPS = 2 * 256 * 128 * 2048 + 5 * 128 * 512


def tile_lookup_pjmix_out_kernel(tc, z, wt, u0, u1, u2, offs, out):
    nc = tc.nc
    features, places = z.shape
    width = out.shape[1]
    half = width // HALVES
    k_blocks = features // P
    z_blocks = z.rearrange("(p h) s -> p h s", p=P)

    with (
        tc.tile_pool(name="held", bufs=1) as held,
        tc.psum_pool(name="psum", bufs=PSUM_BANKS) as psum,
    ):
        projection = held.tile([P, k_blocks, P], BF16, name="projection")
        nc.scalar.dma_start(projection[:], wt.rearrange("(p h) r -> p h r", p=P))

        zeros = held.tile([P, P], BF16, name="zeros")
        nc.vector.memset(zeros[:], 0.0)
        warm = psum.tile([P, half], F32, name="warm", tag="bank")
        for i in range(WARM_MATMULS):
            nc.tensor.matmul(warm[:, :P], zeros[:], zeros[:], start=True, stop=True)

        table = held.tile([P, places], F32, name="table")
        first = 0
        for run in RUNS:
            span = run // 2
            banks = [psum.tile([P, span], F32, name=f"bank{first}_{i}", tag="bank") for i in range(2)]
            for h in range(k_blocks):
                z_part = held.tile([P, run], BF16, name=f"z_part{first}_{h}")
                nc.sync.dma_start(z_part[:], z_blocks[:, h, first : first + run])
                for i, bank in enumerate(banks):
                    nc.tensor.matmul(bank[:], projection[:, h, :], z_part[:, i * span : (i + 1) * span],
                                     start=h == 0, stop=h == k_blocks - 1)
            nc.vector.tensor_copy(table[:, first : first + span], banks[0][:])
            nc.scalar.copy(table[:, first + span : first + run], banks[1][:])
            first += run

        for i in range(KEEP_WARM_MATMULS):
            nc.tensor.matmul(warm[:], zeros[:], z_part[:, :half], start=True, stop=True)

        offsets = held.tile([P, offs.shape[1]], U16, name="offsets")
        mixes = [held.tile([P, width], F32, name=f"mix{d}") for d in range(3)]
        for tile, source in ((mixes[0], u0), (offsets, offs), (mixes[1], u1), (mixes[2], u2)):
            nc.sync.dma_start(tile[:], source)

        def look_up(d, i):
            product = held.tile([P, half], F32, name=f"product{d}_{i}")
            entry = d * width + i * half
            piece = offsets[:, entry // ENTRIES_PER_COLUMN : (entry + half) // ENTRIES_PER_COLUMN]
            nc.vector.tensor_tensor(product[:], table[:].indirect(piece), mixes[d][:, i * half : (i + 1) * half], MULT)
            return product

        identity = held.tile([P, P], F32, name="identity")
        make_identity(nc, identity[:])
        partials = [psum.tile([P, half], F32, name=f"partial{i}", tag="bank") for i in range(HALVES)]
        for d in range(2):
            for i in range(HALVES):
                nc.tensor.matmul(partials[i][:], identity[:], look_up(d, i)[:], start=d == 0, stop=d == 1)

        lasts = [look_up(2, i) for i in range(HALVES)]
        for i in range(HALVES):
            total = held.tile([P, half], F32, name=f"total{i}")
            nc.vector.tensor_tensor(total[:], partials[i][:], lasts[i][:], ADD)
            nc.sync.dma_start(out[:, i * half : (i + 1) * half], total[:])
